import numpy as np
import ml_dtypes


def mxq(x, axis, fmt="e4m3"):
    dtype, down = {"e4m3": (ml_dtypes.float8_e4m3fn, 7), "e5m2": (ml_dtypes.float8_e5m2, 14)}[fmt]
    v = np.moveaxis(np.asarray(x, np.float32).astype(ml_dtypes.bfloat16).astype(np.float64), axis, -1)
    blocks = v.reshape(v.shape[:-1] + (-1, 32))
    amax = np.abs(blocks).max(-1, keepdims=True)
    byte = np.maximum(np.where(amax > 0, np.frexp(amax)[1] - 1 + 127, 0) - down, 1)
    scale = np.exp2(byte - 127.0)
    codes = (blocks / scale).astype(np.float32).astype(dtype).astype(np.float64)
    return np.moveaxis((codes * scale).reshape(v.shape), -1, axis)


WIDE = False


def mx_kscale(k):
    if not WIDE:
        return np.ones(k)
    levels = np.array([10, -10, 5, -5, 0])
    if k % 512:
        return np.exp2(np.random.permutation(np.resize(levels, k // 32))).repeat(32)
    a = np.empty((k // 512, 16))
    for p in range(k // 512):
        a[p, :8] = np.random.permutation(np.resize(levels, 8))
        for g in range(8):
            far = levels[np.abs(levels - a[p, g]) >= 10]
            a[p, g + 8] = far[np.random.randint(len(far))]
    return np.exp2(a.ravel()).repeat(32)


def f64(x):
    return np.asarray(x).astype(np.float64)


def striped(idx):
    return np.tile(idx.reshape(-1, 16).T, (8, 1)).astype(np.uint16)


def unstriped(offs):
    return offs[:16].T.reshape(-1).astype(np.int64)


E2M1 = np.array([0.0, 0.5, 1.0, 1.5, 2.0, 3.0, 4.0, 6.0, -0.0, -0.5, -1.0, -1.5, -2.0, -3.0, -4.0, -6.0])


def pack_weight(w, fmt):
    k, n = w.shape
    w = f64(np.asarray(w, np.float32).astype(ml_dtypes.bfloat16)).reshape(k // 32, 32, n)
    amax = np.abs(w).max(1)
    if fmt == "e4m3":
        byte = np.frexp(amax)[1] - 1 + 127 - 7
    else:
        mant, ex = np.frexp(amax / 6.0)
        byte = np.where(mant > 0.5, ex, ex - 1) + 127
    byte = np.clip(np.where(amax > 0, byte, 1), 1, 254)
    scaled = (w * np.exp2(127.0 - byte)[:, None, :]).reshape(k, n).astype(np.float32)
    by_word = np.ascontiguousarray(scaled.reshape(k // 512, 128, 4, n).transpose(0, 1, 3, 2))
    if fmt == "e4m3":
        words = by_word.astype(ml_dtypes.float8_e4m3fn).view(np.uint8)
    else:
        c = by_word.astype(ml_dtypes.float4_e2m1fn).view(np.uint8) & 0xF
        words = (c[..., 0::2] | (c[..., 1::2] << 4)).reshape(k // 512, 128, 2 * n)
    return np.ascontiguousarray(words), np.ascontiguousarray(byte.astype(np.uint8).reshape(k // 512, 16, n))


def unpack_weight(words, scales, fmt):
    g, _, n = scales.shape
    words = np.ascontiguousarray(words).reshape(g, 128, n, -1)
    if fmt == "e4m3":
        vals = words.view(ml_dtypes.float8_e4m3fn).astype(np.float64)
    else:
        nib = np.empty((g, 128, n, 4), np.uint8)
        nib[..., 0::2] = words & 0xF
        nib[..., 1::2] = words >> 4
        vals = E2M1[nib]
    vals = vals * np.repeat(np.exp2(scales.astype(np.float64) - 127.0), 8, axis=1)[..., None]
    return vals.transpose(0, 1, 3, 2).reshape(g * 512, n)


def gelu(v):
    return 0.5 * v * (1.0 + np.tanh(np.sqrt(2.0 / np.pi) * (v + 0.044715 * v**3)))


K, T, S, H, T2, P, M, N = 1536, 2048, 512, 1024, 1024, 256, 512, 768

def setup_inputs():
    n = np.random.standard_normal
    s = mx_kscale(K)[:, None]
    u = mx_kscale(H)[:, None]
    d = mx_kscale(M)[:, None]
    tab_words, tab_scales = pack_weight(n((K, T)) * s, "e4m3")
    w2_words, w2_scales = pack_weight(1.6 * n((H, M)) / np.sqrt(H) / u, "e2m1")
    w4_words, w4_scales = pack_weight(0.8 * n((H, N)) / np.sqrt(H) / u, "e4m3")
    perm = np.random.permutation(T2)
    return {
        "tab_words": tab_words, "tab_scales": tab_scales,
        "offs": striped(np.random.permutation(T)[:S]),
        "offs2": striped(np.random.permutation(T2)[:S]),
        "offs3": striped(perm[:P]),
        "offs4": striped(perm[P:2 * P]),
        "w1": (1.6 * n((K, H)) / np.sqrt(K) / s).astype(np.float32),
        "gain": (np.exp(0.3 * n(H)) * u[:, 0]).astype(np.float32),
        "wgs": np.exp(0.3 * n((128, S))).astype(np.float32),
        "page0": (n((H, T2)) * u).astype(np.float32),
        "w2_words": w2_words, "w2_scales": w2_scales,
        "gain2": (np.exp(0.3 * n(M)) * d[:, 0]).astype(np.float32),
        "w3": (1.4 * n((M, N)) / np.sqrt(M) / d).astype(np.float32),
        "w4_words": w4_words, "w4_scales": w4_scales,
    }

def reference(tab_words, tab_scales, offs, offs2, offs3, offs4, w1, gain, wgs, page0,
              w2_words, w2_scales, gain2, w3, w4_words, w4_scales):
    v = unpack_weight(tab_words, tab_scales, "e4m3")[:, unstriped(offs)]
    h = f64(gain)[:, None] * np.tanh(mxq(f64(w1), 0, "e4m3").T @ v)
    page = f64(page0).copy()
    page[:, unstriped(offs2)] = np.tile(f64(wgs), (H // 128, 1)) * h
    a = page[:, unstriped(offs3)]
    b = page[:, unstriped(offs4)]
    page[:, unstriped(offs3)] = np.maximum(a, b)
    page[:, unstriped(offs4)] = np.minimum(a, b)
    pq = mxq(page, 0, "e4m3")
    f = unpack_weight(w2_words, w2_scales, "e2m1").T @ pq
    x = f64(gain2)[:, None] * (f / (1.0 + np.exp(-f)))
    w4 = unpack_weight(w4_words, w4_scales, "e4m3")
    return mxq(f64(w3), 0, "e4m3").T @ mxq(x, 0, "e4m3") + w4.T @ pq

@@ -1,0 +1,351 @@
+from contextlib import ExitStack
+
+import concourse.mybir as mybir
+
+K, T, S, H, T2, PAIRS, M, N = 1536, 2048, 512, 1024, 1024, 256, 512, 768
+FLOPS = 2 * (K * H * S + H * M * T2 + M * N * T2 + H * N * T2)
+
+F32 = mybir.dt.float32
+BF16 = mybir.dt.bfloat16
+I32 = mybir.dt.int32
+U32 = mybir.dt.uint32
+U16 = mybir.dt.uint16
+U8 = mybir.dt.uint8
+FP8X4 = mybir.dt.float8_e4m3fn_x4
+FP4X4 = mybir.dt.float4_e2m1fn_x4
+ACT = mybir.ActivationFunctionType
+ALU = mybir.AluOpType
+
+P = 128
+PACK = 4
+PASS = P * PACK
+K_PASSES = K // PASS
+H_PASSES = H // PASS
+TILES = H // P
+HALF = T2 // 2
+QUARTER = T2 // 4
+BANKS = 8
+STRIP = T2 // BANKS
+N_TILES = N // P
+
+
+def tile_list_sitter_booking_page_kernel(
+    tc, tab_words, tab_scales, offs, offs2, offs3, offs4, w1, gain, wgs, page0,
+    w2_words, w2_scales, gain2, w3, w4_words, w4_scales, out,
+):
+    nc = tc.nc
+    with ExitStack() as ctx:
+        lists = ctx.enter_context(tc.tile_pool(name="lists", bufs=1))
+        keep = ctx.enter_context(tc.tile_pool(name="keep", bufs=1))
+        ring = ctx.enter_context(tc.tile_pool(name="ring", bufs=2))
+        psum = ctx.enter_context(tc.psum_pool(name="psum", bufs=1))
+
+        def bank(b, shape):
+            return psum.tile(shape, F32, name=f"bank{b}", tag=f"bank{b}")
+
+        idx = lists.tile([P, S // 16], U16, name="idx")
+        idx2 = lists.tile([P, S // 16], U16, name="idx2")
+        idx3 = lists.tile([P, PAIRS // 16], U16, name="idx3")
+        idx4 = lists.tile([P, PAIRS // 16], U16, name="idx4")
+
+        tab_s = keep.tile([P, T], U8, name="tab_s", align_bytes=64)
+        w2_s_raw = keep.tile([P, H_PASSES * M], U8, name="w2_s_raw", align_bytes=64)
+        w4_s = keep.tile([P, N], U8, name="w4_s", align_bytes=64)
+        for plane in (tab_s, w2_s_raw, w4_s):
+            nc.gpsimd.memset(plane[:].bitcast(I32), 0)
+
+        gain_sb = keep.tile([P, H_PASSES, PACK], F32, name="gain_sb")
+
+        tab_w = [keep.tile([P, T], I32, name=f"tab_w{a}") for a in range(K_PASSES)]
+        pages = [keep.tile([P, T2], F32, name=f"page{n}") for n in range(TILES)]
+        wgs_first = keep.tile([P, S], F32, name="wgs_first")
+        wgs_rest = keep.tile([P, (PACK - 1) * S], F32, name="wgs_rest")
+        wgs_rows = wgs.rearrange("(q i) j -> q (i j)", i=PACK)
+        page_rows = page0.rearrange("(b p i) t -> b i p t", b=H_PASSES, i=PACK)
+        w1_raw = {}
+
+        def load_w1(b, a):
+            raw = ring.tile([P, PACK, PASS], F32, name="w1_raw", bufs=4)
+            nc.sync.dma_start(
+                out=raw[:],
+                in_=w1[PASS * a : PASS * (a + 1), PASS * b : PASS * (b + 1)].rearrange("(p j) c -> p j c", j=PACK),
+            )
+            w1_raw[b, a] = raw
+
+        def load_page(n):
+            nc.sync.dma_start(out=pages[n][:], in_=page_rows[n // PACK, n % PACK])
+
+        nc.sync.dma_start(idx[:], offs)
+        for a in range(K_PASSES):
+            load_w1(0, a)
+            nc.sync.dma_start(out=tab_w[a][:], in_=tab_words[a].rearrange("p t i -> p (t i)").bitcast(I32))
+            if a == 0:
+                for q in range(4):
+                    nc.sync.dma_start(
+                        out=tab_s[32 * q : 32 * q + 4 * K_PASSES, :].bitcast(I32),
+                        in_=tab_scales[:, 4 * q : 4 * q + 4, :].bitcast(I32),
+                    )
+        nc.sync.dma_start(out=gain_sb[:], in_=gain.rearrange("(b p i) -> p b i", b=H_PASSES, i=PACK))
+        nc.sync.dma_start(idx2[:], offs2)
+        for q in range(4):
+            nc.sync.dma_start(out=wgs_first[32 * q : 32 * (q + 1), :], in_=wgs_rows[:, 0:S])
+        load_page(0)
+        nc.sync.dma_start(idx3[:], offs3)
+        nc.sync.dma_start(idx4[:], offs4)
+        for q in range(4):
+            nc.sync.dma_start(out=wgs_rest[32 * q : 32 * (q + 1), :], in_=wgs_rows[:, S : PACK * S])
+        load_page(1)
+        for a in range(K_PASSES):
+            load_w1(1, a)
+        load_page(2)
+        load_page(3)
+
+        w3_raw = keep.tile([P, PACK, N], F32, name="w3_raw", tag="w3_raw_x", align_bytes=64)
+        w3_rows = w3.rearrange("(g i q) n -> i g q n", i=PACK, q=8)
+        for i in range(PACK):
+            nc.sync.dma_start(out=w3_raw[:, i, :], in_=w3_rows[i])
+        w2_w_raw = keep.tile([P, H_PASSES * 2 * M], U8, name="w2_w_raw", align_bytes=64)
+        nc.sync.dma_start(
+            out=w2_w_raw[:].bitcast(I32).rearrange("p (a c) -> p a c", a=H_PASSES),
+            in_=w2_words.bitcast(I32).rearrange("a p c -> p a c"),
+        )
+        w4_w = keep.tile([P, H_PASSES * N], U32, name="w4_w", align_bytes=64)
+        nc.sync.dma_start(
+            out=w4_w[:].bitcast(I32).rearrange("p (a c) -> p a c", a=H_PASSES),
+            in_=w4_words.rearrange("a p c i -> p a (c i)").bitcast(I32),
+        )
+        for q in range(4):
+            nc.sync.dma_start(
+                out=w2_s_raw[32 * q : 32 * q + 4, :].bitcast(I32).rearrange("r (a c) -> r a c", a=H_PASSES),
+                in_=w2_scales[:, 4 * q : 4 * q + 4, :].bitcast(I32).rearrange("a r c -> r a c"),
+            )
+            nc.sync.dma_start(
+                out=w4_s[32 * q : 32 * q + 4 * H_PASSES, :].bitcast(I32),
+                in_=w4_scales[:, 4 * q : 4 * q + 4, :].bitcast(I32),
+            )
+        gain2_raw = keep.tile([P, PACK, 8], F32, name="gain2_raw")
+        gain2_rows = gain2.rearrange("(g i q) -> i g q", i=PACK, q=8)
+        with nc.allow_non_contiguous_dma(reason="one gain for each partition"):
+            for i in range(PACK):
+                nc.sync.dma_start(out=gain2_raw[:, i, 0:1], in_=gain2_rows[i])
+        for n in range(4, TILES):
+            load_page(n)
+
+        v_s = keep.tile([P, S], U8, name="v_s", align_bytes=64)
+        nc.vector.tensor_copy(v_s[:], tab_s[:].indirect(idx[:]))
+        v_w = [keep.tile([P, S], U32, name=f"v_w{a}", align_bytes=64) for a in range(K_PASSES)]
+        w1_w, w1_s = {}, {}
+
+        def group_w1(b, a, engine_copy):
+            grouped = ring.tile([P, PACK * PASS], BF16, name="grouped", tag="grouped", bufs=3, align_bytes=64)
+            engine_copy(
+                out=grouped[:].rearrange("p (t m j) -> p m j t", t=PACK, j=PACK),
+                in_=w1_raw[b, a][:].rearrange("p j (m t) -> p m j t", t=PACK),
+            )
+            return grouped
+
+        def quantize_w1(b, a, grouped):
+            w1_w[b, a] = keep.tile([P, PASS], U32, name=f"w1_w{b}{a}", tag=f"w1_w{b}{a}", align_bytes=64)
+            w1_s[b, a] = keep.tile([P, PASS], U8, name=f"w1_s{b}{a}", align_bytes=64)
+            nc.vector.quantize_mx(out=w1_w[b, a][:].bitcast(FP8X4), scales=w1_s[b, a][:], in_=grouped[:])
+
+        def first_product(n, a, acc):
+            b, i = divmod(n, PACK)
+            cols = slice(P * i, P * (i + 1))
+            nc.tensor.matmul_mx(
+                out=acc[:], lhsT=w1_w[b, a][:, cols].bitcast(FP8X4), lhsT_scale=w1_s[b, a][:, cols],
+                rhs=v_w[a][:].bitcast(FP8X4), rhs_scale=v_s[4 * a : P, :],
+                start=(a == 0), stop=(a == K_PASSES - 1),
+            )
+
+        h = {}
+
+        def activate(n, acc):
+            b, i = divmod(n, PACK)
+            squashed = keep.tile([P, S], F32, name="squashed")
+            nc.scalar.activation(out=squashed[:], in_=acc[:], func=ACT.Tanh)
+            h[n] = keep.tile([P, S], F32, name=f"h{n}", tag=f"h_out{n}")
+            nc.scalar.activation(out=h[n][:], in_=squashed[:], func=ACT.Copy, scale=gain_sb[:, b, i : i + 1])
+
+        accs = [bank(n, [P, S]) for n in range(TILES)]
+        for a in range(K_PASSES):
+            grouped = group_w1(0, a, nc.vector.tensor_copy)
+            quantize_w1(0, a, grouped)
+            nc.vector.tensor_copy(v_w[a][:], tab_w[a][:].bitcast(U32).indirect(idx[:]))
+            for n in range(PACK):
+                first_product(n, a, accs[n])
+        for n in range(PACK):
+            activate(n, accs[n])
+        for a in range(K_PASSES):
+            grouped = group_w1(1, a, nc.scalar.copy)
+            quantize_w1(1, a, grouped)
+        for n in range(PACK, TILES):
+            for a in range(K_PASSES):
+                first_product(n, a, accs[n])
+            activate(n, accs[n])
+
+        w3_grouped = keep.tile([P, N * PACK], BF16, name="w3_grouped", align_bytes=64)
+        nc.scalar.copy(
+            out=w3_grouped[:].rearrange("p (c e t) -> p c t e", e=4, t=PACK),
+            in_=w3_raw[:].rearrange("p t (c e) -> p c t e", e=4),
+        )
+        w3_w = keep.tile([P, N], U32, name="w3_w", align_bytes=64)
+        w3_s = keep.tile([P, N], U8, name="w3_s", align_bytes=64)
+        for c0, c1 in ((0, 512), (512, N)):
+            nc.vector.quantize_mx(
+                out=w3_w[:, c0:c1].bitcast(FP8X4), scales=w3_s[:, c0:c1], in_=w3_grouped[:, PACK * c0 : PACK * c1]
+            )
+        w2_w = keep.tile([P, H_PASSES * 2 * M], U8, name="w2_w", align_bytes=64)
+        w2_s = keep.tile([P, H_PASSES * M], U8, name="w2_s", align_bytes=64)
+        for dealt, raw in ((w2_w, w2_w_raw), (w2_s, w2_s_raw)):
+            nc.scalar.copy(
+                out=dealt[:].bitcast(U32).rearrange("p (a i g w) -> p a i g w", a=H_PASSES, i=PACK, g=16),
+                in_=raw[:].bitcast(U32).rearrange("p (a g i w) -> p a i g w", a=H_PASSES, i=PACK, g=16),
+            )
+
+        gain2_sb = keep.tile([P, PACK], F32, name="gain2_sb")
+        nc.scalar.copy(out=gain2_sb[:], in_=gain2_raw[:, :, 0])
+
+        picked, ordered = {}, {}
+        rounded = {}
+        for half in range(2):
+            rounded[0, half] = keep.tile([P, HALF, PACK], BF16, name=f"rounded0{half}", tag=f"w1_w1{half + 1}", align_bytes=64)
+            rounded[1, half] = keep.tile([P, HALF, PACK], BF16, name=f"rounded1{half}", align_bytes=64)
+        b_w, b_s = {}, {}
+
+        def put(n):
+            i = n % PACK
+            weights = wgs_first[:] if i == 0 else wgs_rest[:, S * (i - 1) : S * i]
+            nc.vector.tensor_tensor(pages[n][:].indirect(idx2[:]), h[n][:], weights, ALU.mult)
+
+        def fetch(n):
+            picked[n] = ring.tile([P, 2 * PAIRS], F32, name="picked", tag="picked", align_bytes=64)
+            nc.vector.tensor_copy(picked[n][:, 0:PAIRS], pages[n][:].indirect(idx3[:]))
+            nc.vector.tensor_copy(picked[n][:, PAIRS:], pages[n][:].indirect(idx4[:]))
+
+        def order(n):
+            ordered[n] = ring.tile([P, 2 * PAIRS], F32, name="ordered")
+            nc.vector.tensor_tensor(ordered[n][:, 0:PAIRS], picked[n][:, 0:PAIRS], picked[n][:, PAIRS:], ALU.max)
+            nc.vector.tensor_tensor(ordered[n][:, PAIRS:], picked[n][:, 0:PAIRS], picked[n][:, PAIRS:], ALU.min)
+
+        def put_larger(n):
+            nc.vector.tensor_copy(pages[n][:].indirect(idx3[:]), ordered[n][:, 0:PAIRS])
+
+        def put_smaller(n):
+            nc.vector.tensor_copy(pages[n][:].indirect(idx4[:]), ordered[n][:, PAIRS:])
+
+        def round_page(n):
+            b, i = divmod(n, PACK)
+            for half in range(2):
+                on_vector = b == 1 and half == 0 and i >= 2
+                engine_copy = nc.vector.tensor_copy if on_vector else nc.scalar.copy
+                pieces = 1 if n < TILES - 1 else 4 if on_vector else 2
+                width = HALF // pieces
+                for piece in range(pieces):
+                    c0 = width * piece
+                    engine_copy(
+                        out=rounded[b, half][:, c0 : c0 + width, i],
+                        in_=pages[n][:, HALF * half + c0 : HALF * half + c0 + width],
+                    )
+
+        def quantize_page(b, half, pieces, tag):
+            if tag is None:
+                b_w[b, half] = keep.tile([P, HALF], U32, name=f"b_w{b}{half}", align_bytes=64)
+            else:
+                b_w[b, half] = ring.tile([P, HALF], U32, name=f"b_w{b}{half}", tag=tag, align_bytes=64)
+            b_s[b, half] = keep.tile([P, HALF], U8, name=f"b_s{b}{half}", align_bytes=64)
+            width = HALF // pieces
+            for piece in range(pieces):
+                cols = slice(width * piece, width * (piece + 1))
+                nc.vector.quantize_mx(
+                    out=b_w[b, half][:, cols].bitcast(FP8X4), scales=b_s[b, half][:, cols],
+                    in_=rounded[b, half][:, cols, :].rearrange("p c i -> p (c i)"),
+                )
+
+        put(0)
+        for n in range(TILES):
+            if n > 0:
+                put_larger(n - 1)
+            fetch(n)
+            if n > 0:
+                put_smaller(n - 1)
+                round_page(n - 1)
+            order(n)
+            if n + 1 < TILES:
+                put(n + 1)
+        last = TILES - 1
+        quantize_page(0, 0, 1, "picked")
+        put_larger(last)
+        quantize_page(0, 1, 1, "picked")
+        put_smaller(last)
+        round_page(last)
+
+        f_banks = [bank(s, [P, PACK, STRIP]) for s in range(BANKS)]
+
+        def second_product(s, b):
+            half, c0 = divmod(STRIP * s, HALF)
+            cols = slice(c0, c0 + STRIP)
+            for i in range(PACK):
+                m0 = M * b + P * i
+                nc.tensor.matmul_mx(
+                    out=f_banks[s][:, i, :],
+                    lhsT=w2_w[:, 2 * m0 : 2 * (m0 + P)].bitcast(FP4X4), lhsT_scale=w2_s[:, m0 : m0 + P],
+                    rhs=b_w[b, half][:, cols].bitcast(FP8X4), rhs_scale=b_s[b, half][:, cols],
+                    start=(b == 0 and i == 0), stop=(b == H_PASSES - 1 and i == PACK - 1),
+                )
+
+        for s in range(BANKS):
+            second_product(s, 0)
+        quantize_page(1, 0, 4, None)
+        quantize_page(1, 1, 2, None)
+        x_rounded = keep.tile([P, T2 * PACK], BF16, name="x_rounded", tag="w3_raw_x", align_bytes=64)
+        x_w = [keep.tile([P, HALF], U32, name=f"x_w{half}", align_bytes=64) for half in range(2)]
+        x_s = [keep.tile([P, HALF], U8, name=f"x_s{half}", align_bytes=64) for half in range(2)]
+        for s in range(BANKS):
+            second_product(s, 1)
+            silu = ring.tile([P, STRIP, PACK], F32, name="silu", tag="grouped", bufs=3, align_bytes=64)
+            nc.scalar.activation(out=silu[:], in_=f_banks[s][:].rearrange("p i c -> p c i"), func=ACT.Silu)
+            nc.vector.tensor_tensor(
+                x_rounded[:, PACK * STRIP * s : PACK * STRIP * (s + 1)].rearrange("p (c i) -> p c i", i=PACK),
+                silu[:], gain2_sb[:].unsqueeze(1).to_broadcast([P, STRIP, PACK]), ALU.mult,
+            )
+            if s % 2 == 1:
+                half, c0 = divmod(STRIP * (s - 1), HALF)
+                cols = slice(c0, c0 + QUARTER)
+                nc.vector.quantize_mx(
+                    out=x_w[half][:, cols].bitcast(FP8X4), scales=x_s[half][:, cols],
+                    in_=x_rounded[:, PACK * STRIP * (s - 1) : PACK * STRIP * (s + 1)],
+                )
+
+        out_banks = {}
+
+        def page_passes(u):
+            half, nt = divmod(u, N_TILES)
+            out_banks[u] = bank(u % BANKS, [P, HALF])
+            for b in range(H_PASSES):
+                nc.tensor.matmul_mx(
+                    out=out_banks[u][:], lhsT=w4_w[:, N * b + P * nt : N * b + P * (nt + 1)].bitcast(FP8X4),
+                    lhsT_scale=w4_s[4 * b : P, P * nt : P * (nt + 1)],
+                    rhs=b_w[b, half][:].bitcast(FP8X4), rhs_scale=b_s[b, half][:],
+                    start=(b == 0), stop=False,
+                )
+
+        def finish(u):
+            half, nt = divmod(u, N_TILES)
+            cols = slice(P * nt, P * (nt + 1))
+            nc.tensor.matmul_mx(
+                out=out_banks[u][:], lhsT=w3_w[:, cols].bitcast(FP8X4), lhsT_scale=w3_s[:, cols],
+                rhs=x_w[half][:].bitcast(FP8X4), rhs_scale=x_s[half][:], start=False, stop=True,
+            )
+            staged = keep.tile([P, HALF], F32, name="staged", tag=f"h_out{u % TILES}")
+            engine_copy = nc.scalar.copy if u < 4 or u % 2 == 1 else nc.vector.tensor_copy
+            engine_copy(out=staged[:], in_=out_banks[u][:])
+            nc.sync.dma_start(out=out[cols, HALF * half : HALF * (half + 1)], in_=staged[:])
+
+        for u in range(N_TILES):
+            page_passes(u)
+        for u in range(N_TILES):
+            finish(u)
+        for u in range(N_TILES, 2 * N_TILES):
+            page_passes(u)
+            finish(u)

@@ -49,35 +49,32 @@ def tile_list_sitter_booking_page_kernel(
         idx4 = lists.tile([P, PAIRS // 16], U16, name="idx4")
 
         tab_s = keep.tile([P, T], U8, name="tab_s", align_bytes=64)
-        w2_s_raw = keep.tile([P, H_PASSES * M], U8, name="w2_s_raw", align_bytes=64)
+        w2_s_raw = keep.tile([P, H_PASSES * M], U8, name="w2_s_raw", tag="plain1", align_bytes=64)
         w4_s = keep.tile([P, N], U8, name="w4_s", align_bytes=64)
         for plane in (tab_s, w2_s_raw, w4_s):
             nc.gpsimd.memset(plane[:].bitcast(I32), 0)
 
-        gain_sb = keep.tile([P, H_PASSES, PACK], F32, name="gain_sb")
-
         tab_w = [keep.tile([P, T], I32, name=f"tab_w{a}") for a in range(K_PASSES)]
         pages = [keep.tile([P, T2], F32, name=f"page{n}") for n in range(TILES)]
-        wgs_first = keep.tile([P, S], F32, name="wgs_first")
-        wgs_rest = keep.tile([P, (PACK - 1) * S], F32, name="wgs_rest")
-        wgs_rows = wgs.rearrange("(q i) j -> q (i j)", i=PACK)
-        page_rows = page0.rearrange("(b p i) t -> b i p t", b=H_PASSES, i=PACK)
-        w1_raw = {}
+        dealt_rows = page0[PASS:H, :].rearrange("(p i) t -> i p t", i=PACK)
+        w1_rows = w1.rearrange("(a p j) c -> a p j c", a=K_PASSES, j=PACK)
+        w1_narrow = [keep.tile([P, K_PASSES * PASS], F32, name=f"w1_narrow{n}", tag=f"w1_narrow{n}", align_bytes=64) for n in range(PACK)]
+        w1_wide = [keep.tile([P, PACK * PASS], F32, name=f"w1_wide{a}", tag=f"w1_wide{a}", align_bytes=64) for a in range(K_PASSES)]
 
-        def load_w1(b, a):
-            raw = ring.tile([P, PACK, PASS], F32, name="w1_raw", bufs=4)
-            nc.sync.dma_start(
-                out=raw[:],
-                in_=w1[PASS * a : PASS * (a + 1), PASS * b : PASS * (b + 1)].rearrange("(p j) c -> p j c", j=PACK),
-            )
-            w1_raw[b, a] = raw
+        def load_narrow(n):
+            for a in range(K_PASSES):
+                nc.sync.dma_start(
+                    out=w1_narrow[n][:, PASS * a : PASS * (a + 1)].rearrange("p (j c) -> p j c", j=PACK),
+                    in_=w1_rows[a, :, :, P * n : P * (n + 1)],
+                )
 
         def load_page(n):
-            nc.sync.dma_start(out=pages[n][:], in_=page_rows[n // PACK, n % PACK])
+            rows = page0[P * n : P * (n + 1), :] if n < PACK else dealt_rows[n - PACK]
+            nc.sync.dma_start(out=pages[n][:], in_=rows)
 
         nc.sync.dma_start(idx[:], offs)
+        load_narrow(0)
         for a in range(K_PASSES):
-            load_w1(0, a)
             nc.sync.dma_start(out=tab_w[a][:], in_=tab_words[a].rearrange("p t i -> p (t i)").bitcast(I32))
             if a == 0:
                 for q in range(4):
@@ -85,40 +82,42 @@ def tile_list_sitter_booking_page_kernel(
                         out=tab_s[32 * q : 32 * q + 4 * K_PASSES, :].bitcast(I32),
                         in_=tab_scales[:, 4 * q : 4 * q + 4, :].bitcast(I32),
                     )
-        nc.sync.dma_start(out=gain_sb[:], in_=gain.rearrange("(b p i) -> p b i", b=H_PASSES, i=PACK))
+        gain_sb = keep.tile([P, H_PASSES, 2 * PACK], F32, name="gain_sb")
+        with nc.allow_non_contiguous_dma(reason="one gain for each partition and tile"):
+            nc.sync.dma_start(out=gain_sb[:, 0, 0:PACK], in_=gain[0:PASS].rearrange("(n p) -> p n", p=P))
         nc.sync.dma_start(idx2[:], offs2)
-        for q in range(4):
-            nc.sync.dma_start(out=wgs_first[32 * q : 32 * (q + 1), :], in_=wgs_rows[:, 0:S])
+        wgs_plain = keep.tile([P, S], F32, name="wgs_plain")
+        nc.sync.dma_start(out=wgs_plain[:], in_=wgs)
         load_page(0)
         nc.sync.dma_start(idx3[:], offs3)
         nc.sync.dma_start(idx4[:], offs4)
-        for q in range(4):
-            nc.sync.dma_start(out=wgs_rest[32 * q : 32 * (q + 1), :], in_=wgs_rows[:, S : PACK * S])
-        load_page(1)
+        for n in range(1, PACK):
+            load_narrow(n)
+            load_page(n)
         for a in range(K_PASSES):
-            load_w1(1, a)
-        load_page(2)
-        load_page(3)
-
-        w3_raw = keep.tile([P, PACK, N], F32, name="w3_raw", tag="w3_raw_x", align_bytes=64)
+            nc.sync.dma_start(
+                out=w1_wide[a][:].rearrange("p (j c) -> p j c", j=PACK), in_=w1_rows[a, :, :, PASS:H]
+            )
+        nc.sync.dma_start(out=gain_sb[:, 1, 0:PACK], in_=gain[PASS:H].rearrange("(p i) -> p i", i=PACK))
+        wgs_dealt = keep.tile([P, PACK * S], F32, name="wgs_dealt")
+        for q in range(4):
+            nc.sync.dma_start(
+                out=wgs_dealt[32 * q : 32 * (q + 1), :], in_=wgs.rearrange("(r i) j -> r (i j)", i=PACK)
+            )
+        load_page(PACK)
+        w3_raw = keep.tile([P, PACK * N], F32, name="w3_raw", tag="w3_raw_x", align_bytes=64)
         w3_rows = w3.rearrange("(g i q) n -> i g q n", i=PACK, q=8)
         for i in range(PACK):
-            nc.sync.dma_start(out=w3_raw[:, i, :], in_=w3_rows[i])
-        w2_w_raw = keep.tile([P, H_PASSES * 2 * M], U8, name="w2_w_raw", align_bytes=64)
-        nc.sync.dma_start(
-            out=w2_w_raw[:].bitcast(I32).rearrange("p (a c) -> p a c", a=H_PASSES),
-            in_=w2_words.bitcast(I32).rearrange("a p c -> p a c"),
-        )
+            nc.sync.dma_start(out=w3_raw[:, N * i : N * (i + 1)], in_=w3_rows[i])
+        for n in range(PACK + 1, TILES):
+            load_page(n)
+
         w4_w = keep.tile([P, H_PASSES * N], U32, name="w4_w", align_bytes=64)
         nc.sync.dma_start(
             out=w4_w[:].bitcast(I32).rearrange("p (a c) -> p a c", a=H_PASSES),
             in_=w4_words.rearrange("a p c i -> p a (c i)").bitcast(I32),
         )
         for q in range(4):
-            nc.sync.dma_start(
-                out=w2_s_raw[32 * q : 32 * q + 4, :].bitcast(I32).rearrange("r (a c) -> r a c", a=H_PASSES),
-                in_=w2_scales[:, 4 * q : 4 * q + 4, :].bitcast(I32).rearrange("a r c -> r a c"),
-            )
             nc.sync.dma_start(
                 out=w4_s[32 * q : 32 * q + 4 * H_PASSES, :].bitcast(I32),
                 in_=w4_scales[:, 4 * q : 4 * q + 4, :].bitcast(I32),
@@ -128,73 +127,109 @@ def tile_list_sitter_booking_page_kernel(
         with nc.allow_non_contiguous_dma(reason="one gain for each partition"):
             for i in range(PACK):
                 nc.sync.dma_start(out=gain2_raw[:, i, 0:1], in_=gain2_rows[i])
-        for n in range(4, TILES):
-            load_page(n)
+        for q in range(4):
+            nc.sync.dma_start(
+                out=w2_s_raw[32 * q : 32 * q + 4, :].bitcast(I32).rearrange("r (a c) -> r a c", a=H_PASSES),
+                in_=w2_scales[:, 4 * q : 4 * q + 4, :].bitcast(I32).rearrange("a r c -> r a c"),
+            )
+        w2_w_raw = keep.tile([P, H_PASSES * 2 * M], U8, name="w2_w_raw", tag="plain0", align_bytes=64)
+        nc.sync.dma_start(
+            out=w2_w_raw[:].bitcast(I32).rearrange("p (a c) -> p a c", a=H_PASSES),
+            in_=w2_words.bitcast(I32).rearrange("a p c -> p a c"),
+        )
 
         v_s = keep.tile([P, S], U8, name="v_s", align_bytes=64)
         nc.vector.tensor_copy(v_s[:], tab_s[:].indirect(idx[:]))
         v_w = [keep.tile([P, S], U32, name=f"v_w{a}", align_bytes=64) for a in range(K_PASSES)]
-        w1_w, w1_s = {}, {}
+        stationary = {}
 
-        def group_w1(b, a, engine_copy):
+        def quantize_narrow(n):
+            grouped = ring.tile([P, K_PASSES * PASS], BF16, name="grouped", tag="grouped", bufs=3, align_bytes=64)
+            for a in range(K_PASSES):
+                cols = slice(PASS * a, PASS * (a + 1))
+                nc.scalar.copy(
+                    out=grouped[:, cols].rearrange("p (c e j) -> p c j e", e=4, j=PACK),
+                    in_=w1_narrow[n][:, cols].rearrange("p (j c e) -> p c j e", e=4, j=PACK),
+                )
+            words = keep.tile([P, K_PASSES * P], U32, name=f"w1_w_narrow{n}", align_bytes=64)
+            scales = keep.tile([P, K_PASSES * P], U8, name=f"w1_s_narrow{n}", align_bytes=64)
+            nc.vector.quantize_mx(out=words[:].bitcast(FP8X4), scales=scales[:], in_=grouped[:])
+            for a in range(K_PASSES):
+                stationary[n, a] = (words[:, P * a : P * (a + 1)], scales[:, P * a : P * (a + 1)])
+
+        def quantize_wide(a):
             grouped = ring.tile([P, PACK * PASS], BF16, name="grouped", tag="grouped", bufs=3, align_bytes=64)
-            engine_copy(
+            nc.scalar.copy(
                 out=grouped[:].rearrange("p (t m j) -> p m j t", t=PACK, j=PACK),
-                in_=w1_raw[b, a][:].rearrange("p j (m t) -> p m j t", t=PACK),
+                in_=w1_wide[a][:].rearrange("p (j m t) -> p m j t", j=PACK, t=PACK),
             )
-            return grouped
+            words = keep.tile([P, PASS], U32, name=f"w1_w_wide{a}", tag=f"w1_w_wide{a}", align_bytes=64)
+            scales = keep.tile([P, PASS], U8, name=f"w1_s_wide{a}", align_bytes=64)
+            nc.vector.quantize_mx(out=words[:].bitcast(FP8X4), scales=scales[:], in_=grouped[:])
+            for i in range(PACK):
+                stationary[PACK + i, a] = (words[:, P * i : P * (i + 1)], scales[:, P * i : P * (i + 1)])
 
-        def quantize_w1(b, a, grouped):
-            w1_w[b, a] = keep.tile([P, PASS], U32, name=f"w1_w{b}{a}", tag=f"w1_w{b}{a}", align_bytes=64)
-            w1_s[b, a] = keep.tile([P, PASS], U8, name=f"w1_s{b}{a}", align_bytes=64)
-            nc.vector.quantize_mx(out=w1_w[b, a][:].bitcast(FP8X4), scales=w1_s[b, a][:], in_=grouped[:])
-
-        def first_product(n, a, acc):
-            b, i = divmod(n, PACK)
-            cols = slice(P * i, P * (i + 1))
+        def first_product(n, a, acc, entries):
+            words, scales = stationary[n, a]
             nc.tensor.matmul_mx(
-                out=acc[:], lhsT=w1_w[b, a][:, cols].bitcast(FP8X4), lhsT_scale=w1_s[b, a][:, cols],
-                rhs=v_w[a][:].bitcast(FP8X4), rhs_scale=v_s[4 * a : P, :],
+                out=acc[:], lhsT=words.bitcast(FP8X4), lhsT_scale=scales,
+                rhs=v_w[a][:, entries].bitcast(FP8X4), rhs_scale=v_s[4 * a : P, entries],
                 start=(a == 0), stop=(a == K_PASSES - 1),
             )
 
-        h = {}
+        squashed = [keep.tile([P, S], F32, name=f"squashed{n}", tag=f"squashed{n}") for n in range(TILES)]
+        h_home = {1: w1_narrow[2], 2: w1_narrow[3], 3: w1_wide[K_PASSES - 1], 5: w3_raw}
+        h = [h_home[n][:, 0:S] if n in h_home else keep.tile([P, S], F32, name=f"h{n}")[:] for n in range(TILES)]
 
-        def activate(n, acc):
+        def activate(n, acc, entries):
             b, i = divmod(n, PACK)
-            squashed = keep.tile([P, S], F32, name="squashed")
-            nc.scalar.activation(out=squashed[:], in_=acc[:], func=ACT.Tanh)
-            h[n] = keep.tile([P, S], F32, name=f"h{n}", tag=f"h_out{n}")
-            nc.scalar.activation(out=h[n][:], in_=squashed[:], func=ACT.Copy, scale=gain_sb[:, b, i : i + 1])
+            nc.scalar.activation(out=squashed[n][:, entries], in_=acc[:], func=ACT.Tanh)
+            nc.scalar.activation(
+                out=h[n][:, entries], in_=squashed[n][:, entries], func=ACT.Copy, scale=gain_sb[:, b, i : i + 1]
+            )
 
-        accs = [bank(n, [P, S]) for n in range(TILES)]
-        for a in range(K_PASSES):
-            grouped = group_w1(0, a, nc.vector.tensor_copy)
-            quantize_w1(0, a, grouped)
-            nc.vector.tensor_copy(v_w[a][:], tab_w[a][:].bitcast(U32).indirect(idx[:]))
-            for n in range(PACK):
-                first_product(n, a, accs[n])
-        for n in range(PACK):
-            activate(n, accs[n])
-        for a in range(K_PASSES):
-            grouped = group_w1(1, a, nc.scalar.copy)
-            quantize_w1(1, a, grouped)
-        for n in range(PACK, TILES):
+        def new_records(n):
+            acc = bank(n, [P, S])
             for a in range(K_PASSES):
-                first_product(n, a, accs[n])
-            activate(n, accs[n])
+                first_product(n, a, acc, whole)
+            activate(n, acc, whole)
 
-        w3_grouped = keep.tile([P, N * PACK], BF16, name="w3_grouped", align_bytes=64)
+        whole = slice(0, S)
+        halves = [slice(0, S // 2), slice(S // 2, S)]
+        quantize_narrow(0)
+        first_banks = [bank(0, [P, S // 2]), bank(BANKS - 1, [P, S // 2])]
+        for a in range(K_PASSES):
+            for entries in halves if a == K_PASSES - 1 else [whole]:
+                nc.vector.tensor_copy(
+                    v_w[a][:, entries],
+                    tab_w[a][:].bitcast(U32).indirect(idx[:, entries.start // 16 : entries.stop // 16]),
+                )
+            for acc, entries in zip(first_banks, halves):
+                first_product(0, a, acc, entries)
+        for acc, entries in zip(first_banks, halves):
+            activate(0, acc, entries)
+        quantize_narrow(1)
+        for n in range(2, PACK):
+            quantize_narrow(n)
+            new_records(n - 1)
+        for a in range(K_PASSES):
+            quantize_wide(a)
+        new_records(PACK - 1)
+        new_records(PACK)
+        w3_grouped = keep.tile([P, N * PACK], BF16, name="w3_grouped", tag="w1_narrow0", align_bytes=64)
         nc.scalar.copy(
             out=w3_grouped[:].rearrange("p (c e t) -> p c t e", e=4, t=PACK),
-            in_=w3_raw[:].rearrange("p t (c e) -> p c t e", e=4),
+            in_=w3_raw[:].rearrange("p (t c e) -> p c t e", e=4, t=PACK),
         )
         w3_w = keep.tile([P, N], U32, name="w3_w", align_bytes=64)
         w3_s = keep.tile([P, N], U8, name="w3_s", align_bytes=64)
-        for c0, c1 in ((0, 512), (512, N)):
+        for c0, c1 in ((0, PASS), (PASS, N)):
             nc.vector.quantize_mx(
                 out=w3_w[:, c0:c1].bitcast(FP8X4), scales=w3_s[:, c0:c1], in_=w3_grouped[:, PACK * c0 : PACK * c1]
             )
+        for n in range(PACK + 1, TILES):
+            new_records(n)
+
         w2_w = keep.tile([P, H_PASSES * 2 * M], U8, name="w2_w", align_bytes=64)
         w2_s = keep.tile([P, H_PASSES * M], U8, name="w2_s", align_bytes=64)
         for dealt, raw in ((w2_w, w2_w_raw), (w2_s, w2_s_raw)):
@@ -207,24 +242,29 @@ def tile_list_sitter_booking_page_kernel(
         nc.scalar.copy(out=gain2_sb[:], in_=gain2_raw[:, :, 0])
 
         picked, ordered = {}, {}
-        rounded = {}
-        for half in range(2):
-            rounded[0, half] = keep.tile([P, HALF, PACK], BF16, name=f"rounded0{half}", tag=f"w1_w1{half + 1}", align_bytes=64)
-            rounded[1, half] = keep.tile([P, HALF, PACK], BF16, name=f"rounded1{half}", align_bytes=64)
+        planes = keep.tile([P, PACK * T2], BF16, name="planes", tag="w1_wide0", align_bytes=64)
+        rounded_first = keep.tile([P, T2, PACK], BF16, name="rounded_first", tag="w1_wide1", align_bytes=64)
+        rounded = {(0, half): rounded_first[:, HALF * half : HALF * (half + 1), :] for half in range(2)}
+        ordered_home = {0: w1_narrow[1][:, 0:S], TILES - 1: planes[:].bitcast(F32)[:, 0:S]}
         b_w, b_s = {}, {}
 
         def put(n):
-            i = n % PACK
-            weights = wgs_first[:] if i == 0 else wgs_rest[:, S * (i - 1) : S * i]
-            nc.vector.tensor_tensor(pages[n][:].indirect(idx2[:]), h[n][:], weights, ALU.mult)
+            weights = wgs_plain[:] if n < PACK else wgs_dealt[:, S * (n - PACK) : S * (n - PACK + 1)]
+            for entries in halves if n == 0 else [whole]:
+                nc.vector.tensor_tensor(
+                    pages[n][:].indirect(idx2[:, entries.start // 16 : entries.stop // 16]),
+                    h[n][:, entries], weights[:, entries], ALU.mult,
+                )
 
-        def fetch(n):
+        def fetch_first(n):
             picked[n] = ring.tile([P, 2 * PAIRS], F32, name="picked", tag="picked", align_bytes=64)
             nc.vector.tensor_copy(picked[n][:, 0:PAIRS], pages[n][:].indirect(idx3[:]))
+
+        def fetch_second(n):
             nc.vector.tensor_copy(picked[n][:, PAIRS:], pages[n][:].indirect(idx4[:]))
 
         def order(n):
-            ordered[n] = ring.tile([P, 2 * PAIRS], F32, name="ordered")
+            ordered[n] = ordered_home[n] if n in ordered_home else squashed[n + 1][:]
             nc.vector.tensor_tensor(ordered[n][:, 0:PAIRS], picked[n][:, 0:PAIRS], picked[n][:, PAIRS:], ALU.max)
             nc.vector.tensor_tensor(ordered[n][:, PAIRS:], picked[n][:, 0:PAIRS], picked[n][:, PAIRS:], ALU.min)
 
@@ -234,19 +274,41 @@ def tile_list_sitter_booking_page_kernel(
         def put_smaller(n):
             nc.vector.tensor_copy(pages[n][:].indirect(idx4[:]), ordered[n][:, PAIRS:])
 
-        def round_page(n):
-            b, i = divmod(n, PACK)
+        def round_plain_page(n):
+            plain = keep.tile([P, T2], BF16, name="plain", tag=f"plain{n % 2}", align_bytes=64)
+            nc.scalar.copy(out=plain[:], in_=pages[n][:])
+            for i in range(PACK):
+                nc.sync.dma_start(out=planes[32 * n : 32 * (n + 1), T2 * i : T2 * (i + 1)], in_=plain[i:P:PACK, :])
+            if n == PACK - 1:
+                for half in range(2):
+                    nc.scalar.copy(
+                        out=rounded[0, half].rearrange("p (c e) i -> p c i e", e=4),
+                        in_=planes[:].rearrange("p (i h c e) -> p h c i e", i=PACK, h=2, e=4)[:, half],
+                    )
+
+        def round_dealt_page(n):
+            i = n - PACK
+            if i == 0:
+                rounded_second = keep.tile([P, T2, PACK], BF16, name="rounded_second", tag="plain1", align_bytes=64)
+                for half in range(2):
+                    rounded[1, half] = rounded_second[:, HALF * half : HALF * (half + 1), :]
             for half in range(2):
-                on_vector = b == 1 and half == 0 and i >= 2
+                on_vector = half == 0 and i >= 2
                 engine_copy = nc.vector.tensor_copy if on_vector else nc.scalar.copy
                 pieces = 1 if n < TILES - 1 else 4 if on_vector else 2
                 width = HALF // pieces
                 for piece in range(pieces):
                     c0 = width * piece
                     engine_copy(
-                        out=rounded[b, half][:, c0 : c0 + width, i],
+                        out=rounded[1, half][:, c0 : c0 + width, i],
                         in_=pages[n][:, HALF * half + c0 : HALF * half + c0 + width],
                     )
+
+        def round_page(n):
+            if n < PACK:
+                round_plain_page(n)
+            else:
+                round_dealt_page(n)
 
         def quantize_page(b, half, pieces, tag):
             if tag is None:
@@ -263,17 +325,25 @@ def tile_list_sitter_booking_page_kernel(
                 )
 
         put(0)
-        for n in range(TILES):
-            if n > 0:
-                put_larger(n - 1)
-            fetch(n)
-            if n > 0:
-                put_smaller(n - 1)
-                round_page(n - 1)
-            order(n)
-            if n + 1 < TILES:
-                put(n + 1)
+        fetch_first(0)
+        fetch_second(0)
+        order(0)
+        put_larger(0)
+        put_smaller(0)
+        round_page(0)
+        put(1)
+        fetch_first(1)
+        fetch_second(1)
+        for n in range(2, TILES):
+            put(n)
+            order(n - 1)
+            fetch_first(n)
+            put_larger(n - 1)
+            fetch_second(n)
+            put_smaller(n - 1)
+            round_page(n - 1)
         last = TILES - 1
+        order(last)
         quantize_page(0, 0, 1, "picked")
         put_larger(last)
         quantize_page(0, 1, 1, "picked")
@@ -337,7 +407,7 @@ def tile_list_sitter_booking_page_kernel(
                 out=out_banks[u][:], lhsT=w3_w[:, cols].bitcast(FP8X4), lhsT_scale=w3_s[:, cols],
                 rhs=x_w[half][:].bitcast(FP8X4), rhs_scale=x_s[half][:], start=False, stop=True,
             )
-            staged = keep.tile([P, HALF], F32, name="staged", tag=f"h_out{u % TILES}")
+            staged = keep.tile([P, HALF], F32, name="staged", tag=f"squashed{u % TILES}")
             engine_copy = nc.scalar.copy if u < 4 or u % 2 == 1 else nc.vector.tensor_copy
             engine_copy(out=staged[:], in_=out_banks[u][:])
             nc.sync.dma_start(out=out[cols, HALF * half : HALF * (half + 1)], in_=staged[:])

@@ -179,7 +179,7 @@ def tile_list_sitter_booking_page_kernel(
 
         squashed = [keep.tile([P, S], F32, name=f"squashed{n}", tag=f"squashed{n}") for n in range(TILES)]
         h_home = {1: w1_narrow[2], 2: w1_narrow[3], 3: w1_wide[K_PASSES - 1], 5: w3_raw}
-        h = [h_home[n][:, 0:S] if n in h_home else keep.tile([P, S], F32, name=f"h{n}")[:] for n in range(TILES)]
+        h = [h_home[n][:, 2 * S : 3 * S] if n in h_home else keep.tile([P, S], F32, name=f"h{n}")[:] for n in range(TILES)]
 
         def activate(n, acc, entries):
             b, i = divmod(n, PACK)
@@ -245,7 +245,7 @@ def tile_list_sitter_booking_page_kernel(
         planes = keep.tile([P, PACK * T2], BF16, name="planes", tag="w1_wide0", align_bytes=64)
         rounded_first = keep.tile([P, T2, PACK], BF16, name="rounded_first", tag="w1_wide1", align_bytes=64)
         rounded = {(0, half): rounded_first[:, HALF * half : HALF * (half + 1), :] for half in range(2)}
-        ordered_home = {0: w1_narrow[1][:, 0:S], TILES - 1: planes[:].bitcast(F32)[:, 0:S]}
+        ordered_home = {0: w1_narrow[1][:, 2 * S : 3 * S], TILES - 1: planes[:].bitcast(F32)[:, 0:S]}
         b_w, b_s = {}, {}
 
         def put(n):

@@ -54,6 +54,10 @@ def tile_list_sitter_booking_page_kernel(
         for plane in (tab_s, w2_s_raw, w4_s):
             nc.gpsimd.memset(plane[:].bitcast(I32), 0)
 
+        warm = keep.tile([P, 16], F32, name="warm")
+        nc.vector.memset(warm[:, 0:1], 0.0)
+        nc.scalar.activation(out=warm[:, 8:9], in_=warm[:, 0:1], func=ACT.Silu)
+
         tab_w = [keep.tile([P, T], I32, name=f"tab_w{a}") for a in range(K_PASSES)]
         pages = [keep.tile([P, T2], F32, name=f"page{n}") for n in range(TILES)]
         dealt_rows = page0[PASS:H, :].rearrange("(p i) t -> i p t", i=PACK)

from contextlib import ExitStack

import concourse.mybir as mybir

K, T, S, H, T2, PAIRS, M, N = 1536, 2048, 512, 1024, 1024, 256, 512, 768
FLOPS = 2 * (K * H * S + H * M * T2 + M * N * T2 + H * N * T2)

F32 = mybir.dt.float32
BF16 = mybir.dt.bfloat16
I32 = mybir.dt.int32
U32 = mybir.dt.uint32
U16 = mybir.dt.uint16
U8 = mybir.dt.uint8
FP8X4 = mybir.dt.float8_e4m3fn_x4
FP4X4 = mybir.dt.float4_e2m1fn_x4
ACT = mybir.ActivationFunctionType
ALU = mybir.AluOpType

P = 128
PACK = 4
PASS = P * PACK
K_PASSES = K // PASS
H_PASSES = H // PASS
TILES = H // P
HALF = T2 // 2
QUARTER = T2 // 4
BANKS = 8
STRIP = T2 // BANKS
N_TILES = N // P


def tile_list_sitter_booking_page_kernel(
    tc, tab_words, tab_scales, offs, offs2, offs3, offs4, w1, gain, wgs, page0,
    w2_words, w2_scales, gain2, w3, w4_words, w4_scales, out,
):
    nc = tc.nc
    with ExitStack() as ctx:
        lists = ctx.enter_context(tc.tile_pool(name="lists", bufs=1))
        keep = ctx.enter_context(tc.tile_pool(name="keep", bufs=1))
        ring = ctx.enter_context(tc.tile_pool(name="ring", bufs=2))
        psum = ctx.enter_context(tc.psum_pool(name="psum", bufs=1))

        def bank(b, shape):
            return psum.tile(shape, F32, name=f"bank{b}", tag=f"bank{b}")

        idx = lists.tile([P, S // 16], U16, name="idx")
        idx2 = lists.tile([P, S // 16], U16, name="idx2")
        idx3 = lists.tile([P, PAIRS // 16], U16, name="idx3")
        idx4 = lists.tile([P, PAIRS // 16], U16, name="idx4")

        tab_s = keep.tile([P, T], U8, name="tab_s", align_bytes=64)
        w2_s_raw = keep.tile([P, H_PASSES * M], U8, name="w2_s_raw", tag="plain1", align_bytes=64)
        w4_s = keep.tile([P, N], U8, name="w4_s", align_bytes=64)
        for plane in (tab_s, w2_s_raw, w4_s):
            nc.gpsimd.memset(plane[:].bitcast(I32), 0)

        warm = keep.tile([P, 16], F32, name="warm")
        nc.vector.memset(warm[:, 0:1], 0.0)
        nc.scalar.activation(out=warm[:, 8:9], in_=warm[:, 0:1], func=ACT.Silu)

        tab_w = [keep.tile([P, T], I32, name=f"tab_w{a}") for a in range(K_PASSES)]
        pages = [keep.tile([P, T2], F32, name=f"page{n}") for n in range(TILES)]
        dealt_rows = page0[PASS:H, :].rearrange("(p i) t -> i p t", i=PACK)
        w1_rows = w1.rearrange("(a p j) c -> a p j c", a=K_PASSES, j=PACK)
        w1_narrow = [keep.tile([P, K_PASSES * PASS], F32, name=f"w1_narrow{n}", tag=f"w1_narrow{n}", align_bytes=64) for n in range(PACK)]
        w1_wide = [keep.tile([P, PACK * PASS], F32, name=f"w1_wide{a}", tag=f"w1_wide{a}", align_bytes=64) for a in range(K_PASSES)]

        def load_narrow(n):
            for a in range(K_PASSES):
                nc.sync.dma_start(
                    out=w1_narrow[n][:, PASS * a : PASS * (a + 1)].rearrange("p (j c) -> p j c", j=PACK),
                    in_=w1_rows[a, :, :, P * n : P * (n + 1)],
                )

        def load_page(n):
            rows = page0[P * n : P * (n + 1), :] if n < PACK else dealt_rows[n - PACK]
            nc.sync.dma_start(out=pages[n][:], in_=rows)

        nc.sync.dma_start(idx[:], offs)
        load_narrow(0)
        for a in range(K_PASSES):
            nc.sync.dma_start(out=tab_w[a][:], in_=tab_words[a].rearrange("p t i -> p (t i)").bitcast(I32))
            if a == 0:
                for q in range(4):
                    nc.sync.dma_start(
                        out=tab_s[32 * q : 32 * q + 4 * K_PASSES, :].bitcast(I32),
                        in_=tab_scales[:, 4 * q : 4 * q + 4, :].bitcast(I32),
                    )
        gain_sb = keep.tile([P, H_PASSES, 2 * PACK], F32, name="gain_sb")
        with nc.allow_non_contiguous_dma(reason="one gain for each partition and tile"):
            nc.sync.dma_start(out=gain_sb[:, 0, 0:PACK], in_=gain[0:PASS].rearrange("(n p) -> p n", p=P))
        nc.sync.dma_start(idx2[:], offs2)
        wgs_plain = keep.tile([P, S], F32, name="wgs_plain")
        nc.sync.dma_start(out=wgs_plain[:], in_=wgs)
        load_page(0)
        nc.sync.dma_start(idx3[:], offs3)
        nc.sync.dma_start(idx4[:], offs4)
        for n in range(1, PACK):
            load_narrow(n)
            load_page(n)
        for a in range(K_PASSES):
            nc.sync.dma_start(
                out=w1_wide[a][:].rearrange("p (j c) -> p j c", j=PACK), in_=w1_rows[a, :, :, PASS:H]
            )
        nc.sync.dma_start(out=gain_sb[:, 1, 0:PACK], in_=gain[PASS:H].rearrange("(p i) -> p i", i=PACK))
        wgs_dealt = keep.tile([P, PACK * S], F32, name="wgs_dealt")
        for q in range(4):
            nc.sync.dma_start(
                out=wgs_dealt[32 * q : 32 * (q + 1), :], in_=wgs.rearrange("(r i) j -> r (i j)", i=PACK)
            )
        load_page(PACK)
        w3_raw = keep.tile([P, PACK * N], F32, name="w3_raw", tag="w3_raw_x", align_bytes=64)
        w3_rows = w3.rearrange("(g i q) n -> i g q n", i=PACK, q=8)
        for i in range(PACK):
            nc.sync.dma_start(out=w3_raw[:, N * i : N * (i + 1)], in_=w3_rows[i])
        for n in range(PACK + 1, TILES):
            load_page(n)

        w4_w = keep.tile([P, H_PASSES * N], U32, name="w4_w", align_bytes=64)
        nc.sync.dma_start(
            out=w4_w[:].bitcast(I32).rearrange("p (a c) -> p a c", a=H_PASSES),
            in_=w4_words.rearrange("a p c i -> p a (c i)").bitcast(I32),
        )
        for q in range(4):
            nc.sync.dma_start(
                out=w4_s[32 * q : 32 * q + 4 * H_PASSES, :].bitcast(I32),
                in_=w4_scales[:, 4 * q : 4 * q + 4, :].bitcast(I32),
            )
        gain2_raw = keep.tile([P, PACK, 8], F32, name="gain2_raw")
        gain2_rows = gain2.rearrange("(g i q) -> i g q", i=PACK, q=8)
        with nc.allow_non_contiguous_dma(reason="one gain for each partition"):
            for i in range(PACK):
                nc.sync.dma_start(out=gain2_raw[:, i, 0:1], in_=gain2_rows[i])
        for q in range(4):
            nc.sync.dma_start(
                out=w2_s_raw[32 * q : 32 * q + 4, :].bitcast(I32).rearrange("r (a c) -> r a c", a=H_PASSES),
                in_=w2_scales[:, 4 * q : 4 * q + 4, :].bitcast(I32).rearrange("a r c -> r a c"),
            )
        w2_w_raw = keep.tile([P, H_PASSES * 2 * M], U8, name="w2_w_raw", tag="plain0", align_bytes=64)
        nc.sync.dma_start(
            out=w2_w_raw[:].bitcast(I32).rearrange("p (a c) -> p a c", a=H_PASSES),
            in_=w2_words.bitcast(I32).rearrange("a p c -> p a c"),
        )

        v_s = keep.tile([P, S], U8, name="v_s", align_bytes=64)
        nc.vector.tensor_copy(v_s[:], tab_s[:].indirect(idx[:]))
        v_w = [keep.tile([P, S], U32, name=f"v_w{a}", align_bytes=64) for a in range(K_PASSES)]
        stationary = {}

        def quantize_narrow(n):
            grouped = ring.tile([P, K_PASSES * PASS], BF16, name="grouped", tag="grouped", bufs=3, align_bytes=64)
            for a in range(K_PASSES):
                cols = slice(PASS * a, PASS * (a + 1))
                nc.scalar.copy(
                    out=grouped[:, cols].rearrange("p (c e j) -> p c j e", e=4, j=PACK),
                    in_=w1_narrow[n][:, cols].rearrange("p (j c e) -> p c j e", e=4, j=PACK),
                )
            words = keep.tile([P, K_PASSES * P], U32, name=f"w1_w_narrow{n}", align_bytes=64)
            scales = keep.tile([P, K_PASSES * P], U8, name=f"w1_s_narrow{n}", align_bytes=64)
            nc.vector.quantize_mx(out=words[:].bitcast(FP8X4), scales=scales[:], in_=grouped[:])
            for a in range(K_PASSES):
                stationary[n, a] = (words[:, P * a : P * (a + 1)], scales[:, P * a : P * (a + 1)])

        def quantize_wide(a):
            grouped = ring.tile([P, PACK * PASS], BF16, name="grouped", tag="grouped", bufs=3, align_bytes=64)
            nc.scalar.copy(
                out=grouped[:].rearrange("p (t m j) -> p m j t", t=PACK, j=PACK),
                in_=w1_wide[a][:].rearrange("p (j m t) -> p m j t", j=PACK, t=PACK),
            )
            words = keep.tile([P, PASS], U32, name=f"w1_w_wide{a}", tag=f"w1_w_wide{a}", align_bytes=64)
            scales = keep.tile([P, PASS], U8, name=f"w1_s_wide{a}", align_bytes=64)
            nc.vector.quantize_mx(out=words[:].bitcast(FP8X4), scales=scales[:], in_=grouped[:])
            for i in range(PACK):
                stationary[PACK + i, a] = (words[:, P * i : P * (i + 1)], scales[:, P * i : P * (i + 1)])

        def first_product(n, a, acc, entries):
            words, scales = stationary[n, a]
            nc.tensor.matmul_mx(
                out=acc[:], lhsT=words.bitcast(FP8X4), lhsT_scale=scales,
                rhs=v_w[a][:, entries].bitcast(FP8X4), rhs_scale=v_s[4 * a : P, entries],
                start=(a == 0), stop=(a == K_PASSES - 1),
            )

        squashed = [keep.tile([P, S], F32, name=f"squashed{n}", tag=f"squashed{n}") for n in range(TILES)]
        h_home = {1: w1_narrow[2], 2: w1_narrow[3], 3: w1_wide[K_PASSES - 1], 5: w3_raw}
        h = [h_home[n][:, 2 * S : 3 * S] if n in h_home else keep.tile([P, S], F32, name=f"h{n}")[:] for n in range(TILES)]

        def activate(n, acc, entries):
            b, i = divmod(n, PACK)
            nc.scalar.activation(out=squashed[n][:, entries], in_=acc[:], func=ACT.Tanh)
            nc.scalar.activation(
                out=h[n][:, entries], in_=squashed[n][:, entries], func=ACT.Copy, scale=gain_sb[:, b, i : i + 1]
            )

        def new_records(n):
            acc = bank(n, [P, S])
            for a in range(K_PASSES):
                first_product(n, a, acc, whole)
            activate(n, acc, whole)

        whole = slice(0, S)
        halves = [slice(0, S // 2), slice(S // 2, S)]
        quantize_narrow(0)
        first_banks = [bank(0, [P, S // 2]), bank(BANKS - 1, [P, S // 2])]
        for a in range(K_PASSES):
            for entries in halves if a == K_PASSES - 1 else [whole]:
                nc.vector.tensor_copy(
                    v_w[a][:, entries],
                    tab_w[a][:].bitcast(U32).indirect(idx[:, entries.start // 16 : entries.stop // 16]),
                )
            for acc, entries in zip(first_banks, halves):
                first_product(0, a, acc, entries)
        for acc, entries in zip(first_banks, halves):
            activate(0, acc, entries)
        quantize_narrow(1)
        for n in range(2, PACK):
            quantize_narrow(n)
            new_records(n - 1)
        for a in range(K_PASSES):
            quantize_wide(a)
        new_records(PACK - 1)
        new_records(PACK)
        w3_grouped = keep.tile([P, N * PACK], BF16, name="w3_grouped", tag="w1_narrow0", align_bytes=64)
        nc.scalar.copy(
            out=w3_grouped[:].rearrange("p (c e t) -> p c t e", e=4, t=PACK),
            in_=w3_raw[:].rearrange("p (t c e) -> p c t e", e=4, t=PACK),
        )
        w3_w = keep.tile([P, N], U32, name="w3_w", align_bytes=64)
        w3_s = keep.tile([P, N], U8, name="w3_s", align_bytes=64)
        for c0, c1 in ((0, PASS), (PASS, N)):
            nc.vector.quantize_mx(
                out=w3_w[:, c0:c1].bitcast(FP8X4), scales=w3_s[:, c0:c1], in_=w3_grouped[:, PACK * c0 : PACK * c1]
            )
        for n in range(PACK + 1, TILES):
            new_records(n)

        w2_w = keep.tile([P, H_PASSES * 2 * M], U8, name="w2_w", align_bytes=64)
        w2_s = keep.tile([P, H_PASSES * M], U8, name="w2_s", align_bytes=64)
        for dealt, raw in ((w2_w, w2_w_raw), (w2_s, w2_s_raw)):
            nc.scalar.copy(
                out=dealt[:].bitcast(U32).rearrange("p (a i g w) -> p a i g w", a=H_PASSES, i=PACK, g=16),
                in_=raw[:].bitcast(U32).rearrange("p (a g i w) -> p a i g w", a=H_PASSES, i=PACK, g=16),
            )

        gain2_sb = keep.tile([P, PACK], F32, name="gain2_sb")
        nc.scalar.copy(out=gain2_sb[:], in_=gain2_raw[:, :, 0])

        picked, ordered = {}, {}
        planes = keep.tile([P, PACK * T2], BF16, name="planes", tag="w1_wide0", align_bytes=64)
        rounded_first = keep.tile([P, T2, PACK], BF16, name="rounded_first", tag="w1_wide1", align_bytes=64)
        rounded = {(0, half): rounded_first[:, HALF * half : HALF * (half + 1), :] for half in range(2)}
        ordered_home = {0: w1_narrow[1][:, 2 * S : 3 * S], TILES - 1: planes[:].bitcast(F32)[:, 0:S]}
        b_w, b_s = {}, {}

        def put(n):
            weights = wgs_plain[:] if n < PACK else wgs_dealt[:, S * (n - PACK) : S * (n - PACK + 1)]
            for entries in halves if n == 0 else [whole]:
                nc.vector.tensor_tensor(
                    pages[n][:].indirect(idx2[:, entries.start // 16 : entries.stop // 16]),
                    h[n][:, entries], weights[:, entries], ALU.mult,
                )

        def fetch_first(n):
            picked[n] = ring.tile([P, 2 * PAIRS], F32, name="picked", tag="picked", align_bytes=64)
            nc.vector.tensor_copy(picked[n][:, 0:PAIRS], pages[n][:].indirect(idx3[:]))

        def fetch_second(n):
            nc.vector.tensor_copy(picked[n][:, PAIRS:], pages[n][:].indirect(idx4[:]))

        def order(n):
            ordered[n] = ordered_home[n] if n in ordered_home else squashed[n + 1][:]
            nc.vector.tensor_tensor(ordered[n][:, 0:PAIRS], picked[n][:, 0:PAIRS], picked[n][:, PAIRS:], ALU.max)
            nc.vector.tensor_tensor(ordered[n][:, PAIRS:], picked[n][:, 0:PAIRS], picked[n][:, PAIRS:], ALU.min)

        def put_larger(n):
            nc.vector.tensor_copy(pages[n][:].indirect(idx3[:]), ordered[n][:, 0:PAIRS])

        def put_smaller(n):
            nc.vector.tensor_copy(pages[n][:].indirect(idx4[:]), ordered[n][:, PAIRS:])

        def round_plain_page(n):
            plain = keep.tile([P, T2], BF16, name="plain", tag=f"plain{n % 2}", align_bytes=64)
            nc.scalar.copy(out=plain[:], in_=pages[n][:])
            for i in range(PACK):
                nc.sync.dma_start(out=planes[32 * n : 32 * (n + 1), T2 * i : T2 * (i + 1)], in_=plain[i:P:PACK, :])
            if n == PACK - 1:
                for half in range(2):
                    nc.scalar.copy(
                        out=rounded[0, half].rearrange("p (c e) i -> p c i e", e=4),
                        in_=planes[:].rearrange("p (i h c e) -> p h c i e", i=PACK, h=2, e=4)[:, half],
                    )

        def round_dealt_page(n):
            i = n - PACK
            if i == 0:
                rounded_second = keep.tile([P, T2, PACK], BF16, name="rounded_second", tag="plain1", align_bytes=64)
                for half in range(2):
                    rounded[1, half] = rounded_second[:, HALF * half : HALF * (half + 1), :]
            for half in range(2):
                on_vector = half == 0 and i >= 2
                engine_copy = nc.vector.tensor_copy if on_vector else nc.scalar.copy
                pieces = 1 if n < TILES - 1 else 4 if on_vector else 2
                width = HALF // pieces
                for piece in range(pieces):
                    c0 = width * piece
                    engine_copy(
                        out=rounded[1, half][:, c0 : c0 + width, i],
                        in_=pages[n][:, HALF * half + c0 : HALF * half + c0 + width],
                    )

        def round_page(n):
            if n < PACK:
                round_plain_page(n)
            else:
                round_dealt_page(n)

        def quantize_page(b, half, pieces, tag):
            if tag is None:
                b_w[b, half] = keep.tile([P, HALF], U32, name=f"b_w{b}{half}", align_bytes=64)
            else:
                b_w[b, half] = ring.tile([P, HALF], U32, name=f"b_w{b}{half}", tag=tag, align_bytes=64)
            b_s[b, half] = keep.tile([P, HALF], U8, name=f"b_s{b}{half}", align_bytes=64)
            width = HALF // pieces
            for piece in range(pieces):
                cols = slice(width * piece, width * (piece + 1))
                nc.vector.quantize_mx(
                    out=b_w[b, half][:, cols].bitcast(FP8X4), scales=b_s[b, half][:, cols],
                    in_=rounded[b, half][:, cols, :].rearrange("p c i -> p (c i)"),
                )

        put(0)
        fetch_first(0)
        fetch_second(0)
        order(0)
        put_larger(0)
        put_smaller(0)
        round_page(0)
        put(1)
        fetch_first(1)
        fetch_second(1)
        for n in range(2, TILES):
            put(n)
            order(n - 1)
            fetch_first(n)
            put_larger(n - 1)
            fetch_second(n)
            put_smaller(n - 1)
            round_page(n - 1)
        last = TILES - 1
        order(last)
        quantize_page(0, 0, 1, "picked")
        put_larger(last)
        quantize_page(0, 1, 1, "picked")
        put_smaller(last)
        round_page(last)

        f_banks = [bank(s, [P, PACK, STRIP]) for s in range(BANKS)]

        def second_product(s, b):
            half, c0 = divmod(STRIP * s, HALF)
            cols = slice(c0, c0 + STRIP)
            for i in range(PACK):
                m0 = M * b + P * i
                nc.tensor.matmul_mx(
                    out=f_banks[s][:, i, :],
                    lhsT=w2_w[:, 2 * m0 : 2 * (m0 + P)].bitcast(FP4X4), lhsT_scale=w2_s[:, m0 : m0 + P],
                    rhs=b_w[b, half][:, cols].bitcast(FP8X4), rhs_scale=b_s[b, half][:, cols],
                    start=(b == 0 and i == 0), stop=(b == H_PASSES - 1 and i == PACK - 1),
                )

        for s in range(BANKS):
            second_product(s, 0)
        quantize_page(1, 0, 4, None)
        quantize_page(1, 1, 2, None)
        x_rounded = keep.tile([P, T2 * PACK], BF16, name="x_rounded", tag="w3_raw_x", align_bytes=64)
        x_w = [keep.tile([P, HALF], U32, name=f"x_w{half}", align_bytes=64) for half in range(2)]
        x_s = [keep.tile([P, HALF], U8, name=f"x_s{half}", align_bytes=64) for half in range(2)]
        for s in range(BANKS):
            second_product(s, 1)
            silu = ring.tile([P, STRIP, PACK], F32, name="silu", tag="grouped", bufs=3, align_bytes=64)
            nc.scalar.activation(out=silu[:], in_=f_banks[s][:].rearrange("p i c -> p c i"), func=ACT.Silu)
            nc.vector.tensor_tensor(
                x_rounded[:, PACK * STRIP * s : PACK * STRIP * (s + 1)].rearrange("p (c i) -> p c i", i=PACK),
                silu[:], gain2_sb[:].unsqueeze(1).to_broadcast([P, STRIP, PACK]), ALU.mult,
            )
            if s % 2 == 1:
                half, c0 = divmod(STRIP * (s - 1), HALF)
                cols = slice(c0, c0 + QUARTER)
                nc.vector.quantize_mx(
                    out=x_w[half][:, cols].bitcast(FP8X4), scales=x_s[half][:, cols],
                    in_=x_rounded[:, PACK * STRIP * (s - 1) : PACK * STRIP * (s + 1)],
                )

        out_banks = {}

        def page_passes(u):
            half, nt = divmod(u, N_TILES)
            out_banks[u] = bank(u % BANKS, [P, HALF])
            for b in range(H_PASSES):
                nc.tensor.matmul_mx(
                    out=out_banks[u][:], lhsT=w4_w[:, N * b + P * nt : N * b + P * (nt + 1)].bitcast(FP8X4),
                    lhsT_scale=w4_s[4 * b : P, P * nt : P * (nt + 1)],
                    rhs=b_w[b, half][:].bitcast(FP8X4), rhs_scale=b_s[b, half][:],
                    start=(b == 0), stop=False,
                )

        def finish(u):
            half, nt = divmod(u, N_TILES)
            cols = slice(P * nt, P * (nt + 1))
            nc.tensor.matmul_mx(
                out=out_banks[u][:], lhsT=w3_w[:, cols].bitcast(FP8X4), lhsT_scale=w3_s[:, cols],
                rhs=x_w[half][:].bitcast(FP8X4), rhs_scale=x_s[half][:], start=False, stop=True,
            )
            staged = keep.tile([P, HALF], F32, name="staged", tag=f"squashed{u % TILES}")
            engine_copy = nc.scalar.copy if u < 4 or u % 2 == 1 else nc.vector.tensor_copy
            engine_copy(out=staged[:], in_=out_banks[u][:])
            nc.sync.dma_start(out=out[cols, HALF * half : HALF * (half + 1)], in_=staged[:])

        for u in range(N_TILES):
            page_passes(u)
        for u in range(N_TILES):
            finish(u)
        for u in range(N_TILES, 2 * N_TILES):
            page_passes(u)
            finish(u)
